import numpy as np
import ml_dtypes


def mxq(x, axis, fmt="e4m3"):
    dtype, down = {"e4m3": (ml_dtypes.float8_e4m3fn, 7), "e5m2": (ml_dtypes.float8_e5m2, 14)}[fmt]
    v = np.moveaxis(np.asarray(x, np.float32).astype(ml_dtypes.bfloat16).astype(np.float64), axis, -1)
    blocks = v.reshape(v.shape[:-1] + (-1, 32))
    amax = np.abs(blocks).max(-1, keepdims=True)
    byte = np.maximum(np.where(amax > 0, np.frexp(amax)[1] - 1 + 127, 0) - down, 1)
    scale = np.exp2(byte - 127.0)
    codes = (blocks / scale).astype(np.float32).astype(dtype).astype(np.float64)
    return np.moveaxis((codes * scale).reshape(v.shape), -1, axis)


WIDE = False


def mx_kscale(k):
    if not WIDE:
        return np.ones(k)
    levels = np.array([10, -10, 5, -5, 0])
    if k % 512:
        return np.exp2(np.random.permutation(np.resize(levels, k // 32))).repeat(32)
    a = np.empty((k // 512, 16))
    for p in range(k // 512):
        a[p, :8] = np.random.permutation(np.resize(levels, 8))
        for g in range(8):
            far = levels[np.abs(levels - a[p, g]) >= 10]
            a[p, g + 8] = far[np.random.randint(len(far))]
    return np.exp2(a.ravel()).repeat(32)


def f64(x):
    return np.asarray(x).astype(np.float64)


def striped(idx):
    return np.tile(np.asarray(idx).reshape(-1, 16).T, (8, 1)).astype(np.uint16)


def unstriped(offs):
    return offs[:16].T.reshape(-1).astype(np.int64)


def striped8(idx):
    return np.asarray(idx).reshape(8, -1, 16).transpose(0, 2, 1).reshape(128, -1).astype(np.uint16)


def unstriped8(offs):
    return offs.reshape(8, 16, -1).transpose(0, 2, 1).reshape(8, -1).astype(np.int64)


def pick8(x, idx, run):
    r = np.arange(len(x))
    return x[r[:, None], idx[r % (8 * run) // run]]


E2M1 = np.array([0.0, 0.5, 1.0, 1.5, 2.0, 3.0, 4.0, 6.0, -0.0, -0.5, -1.0, -1.5, -2.0, -3.0, -4.0, -6.0])


def pack_weight(w, fmt):
    k, n = w.shape
    w = f64(np.asarray(w, np.float32).astype(ml_dtypes.bfloat16)).reshape(k // 32, 32, n)
    amax = np.abs(w).max(1)
    if fmt == "e4m3":
        byte = np.frexp(amax)[1] - 1 + 127 - 7
    else:
        mant, ex = np.frexp(amax / 6.0)
        byte = np.where(mant > 0.5, ex, ex - 1) + 127
    byte = np.clip(np.where(amax > 0, byte, 1), 1, 254)
    scaled = (w * np.exp2(127.0 - byte)[:, None, :]).reshape(k, n).astype(np.float32)
    by_word = np.ascontiguousarray(scaled.reshape(k // 512, 128, 4, n).transpose(0, 1, 3, 2))
    if fmt == "e4m3":
        words = by_word.astype(ml_dtypes.float8_e4m3fn).view(np.uint8)
    else:
        c = by_word.astype(ml_dtypes.float4_e2m1fn).view(np.uint8) & 0xF
        words = (c[..., 0::2] | (c[..., 1::2] << 4)).reshape(k // 512, 128, 2 * n)
    return np.ascontiguousarray(words), np.ascontiguousarray(byte.astype(np.uint8).reshape(k // 512, 16, n))


def unpack_weight(words, scales, fmt):
    g, _, n = scales.shape
    words = np.ascontiguousarray(words).reshape(g, 128, n, -1)
    if fmt == "e4m3":
        vals = words.view(ml_dtypes.float8_e4m3fn).astype(np.float64)
    else:
        nib = np.empty((g, 128, n, 4), np.uint8)
        nib[..., 0::2] = words & 0xF
        nib[..., 1::2] = words >> 4
        vals = E2M1[nib]
    vals = vals * np.repeat(np.exp2(scales.astype(np.float64) - 127.0), 8, axis=1)[..., None]
    return vals.transpose(0, 1, 3, 2).reshape(g * 512, n)


K, J, R, T, F, C, O, N, U = 512, 512, 512, 1024, 1024, 1024, 512, 256, 1024


def setup_inputs():
    n = np.random.standard_normal
    idx = np.random.permutation(T)[:J]
    idx2 = np.random.permutation(F)[:R]
    idx3 = np.stack([np.random.permutation(C)[:J] for _ in range(8)])
    idx4 = np.stack([np.random.permutation(C)[:J] for _ in range(8)])
    idx5 = np.stack([np.random.permutation(C)[:O] for _ in range(8)])
    idx6 = np.stack([np.random.permutation(C)[:O] for _ in range(8)])
    idx7 = np.stack([np.random.permutation(U)[:O] for _ in range(8)])
    fk = mx_kscale(K)
    fr = mx_kscale(R)
    tr = np.ones(F)
    tr[idx2] = fr
    xtp = pack_weight(n((K, T)) * fk[:, None], "e4m3")
    wtp = pack_weight(n((K, F)) * 1 / np.sqrt(K) / fk[:, None] * tr, "e2m1")
    wbp = pack_weight(n((R, N)) * 1 / np.sqrt(R) / fr[:, None], "e4m3")
    return {
        "xt_words": xtp[0],
        "xt_scales": xtp[1],
        "wt_words": wtp[0],
        "wt_scales": wtp[1],
        "sa": (np.random.uniform(0.5, 1.6, (R, 1))).astype(np.float32),
        "sb": (np.random.uniform(0.5, 1.6, (R, 1))).astype(np.float32),
        "wb_words": wbp[0],
        "wb_scales": wbp[1],
        "offs": striped(idx),
        "offs2": striped(idx2),
        "offs3": striped8(idx3),
        "offs4": striped8(idx4),
        "offs5": striped8(idx5),
        "offs6": striped8(idx6),
        "offs7": striped8(idx7),
    }


def reference(xt_words, xt_scales, wt_words, wt_scales, sa, sb, wb_words, wb_scales, offs, offs2, offs3, offs4, offs5, offs6, offs7):
    idx = unstriped(offs)
    idx2 = unstriped(offs2)
    idx3 = unstriped8(offs3)
    idx4 = unstriped8(offs4)
    idx5 = unstriped8(offs5)
    idx6 = unstriped8(offs6)
    idx7 = unstriped8(offs7)
    xtu = unpack_weight(xt_words, xt_scales, "e4m3")
    wtu = unpack_weight(wt_words, wt_scales, "e2m1")
    wbu = unpack_weight(wb_words, wb_scales, "e4m3")
    wtidx2g = wtu[:, idx2]
    xtidxg = xtu[:, idx]
    a = wtidx2g.T @ xtidxg
    g1 = np.pad(a, ((0, 0), (1, 0)))[:, :J]
    g2 = a - g1
    pw = np.zeros((R, C))
    pw[np.arange(R)[:, None], idx3[np.arange(R) % 512 // 64]] = a
    pv = np.zeros((R, C))
    pv[np.arange(R)[:, None], idx4[np.arange(R) % 512 // 64]] = g2
    hid = np.maximum(pick8(pw, idx5, 64) * f64(sa), pick8(pv, idx6, 64) * f64(sb))
    hidq = mxq(hid, 0, "e4m3")
    p = wbu.T @ hidq
    m0 = np.zeros((N, U))
    m0[np.arange(N)[:, None], idx7[np.arange(N) % 128 // 16]] = p
    m1 = np.pad(m0, ((0, 0), (1, 0)))[:, :U]
    y = m0 - m1
    return y

@@ -1,0 +1,219 @@
+from contextlib import ExitStack
+
+import concourse.mybir as mybir
+
+K, J, R, T, F, C, O, N, U = 512, 512, 512, 1024, 1024, 1024, 512, 256, 1024
+FLOPS = 2 * K * R * J + 2 * R * N * O
+
+F32 = mybir.dt.float32
+BF16 = mybir.dt.bfloat16
+I32 = mybir.dt.int32
+U32 = mybir.dt.uint32
+U16 = mybir.dt.uint16
+U8 = mybir.dt.uint8
+FP8X4 = mybir.dt.float8_e4m3fn_x4
+FP4X4 = mybir.dt.float4_e2m1fn_x4
+COPY = mybir.ActivationFunctionType.Copy
+SUB = mybir.AluOpType.subtract
+MAX = mybir.AluOpType.max
+
+P = 128
+PACK = 4
+PAD = 8
+HALF = O // 2
+FIRST_CHUNKS = ((0, 128), (128, 256), (256, 512))
+OUT_CHUNK = 256
+
+
+def entries(lst, lo, hi):
+    return lst[:, lo // 16 : hi // 16]
+
+
+def load_scale_rows(queue, plane, rows):
+    for q in range(4):
+        queue.dma_start(out=plane[32 * q : 32 * q + 4, :].bitcast(I32), in_=rows[4 * q : 4 * q + 4, :].bitcast(I32))
+
+
+def tile_picked_tokens_store_one_changes_one_endsteps_kernel(
+    tc, xt_words, xt_scales, wt_words, wt_scales, sa, sb, wb_words, wb_scales,
+    offs, offs2, offs3, offs4, offs5, offs6, offs7, out,
+):
+    nc = tc.nc
+    with ExitStack() as ctx:
+        keep = ctx.enter_context(tc.tile_pool(name="keep", bufs=1))
+        psum = ctx.enter_context(tc.psum_pool(name="psum", bufs=8))
+
+        def load_list(src, name):
+            tile = keep.tile([P, 32], U16, name=name)
+            nc.sync.dma_start(out=tile[:], in_=src)
+            return tile
+
+        wt_scale_win = keep.tile([P, F], U8, name="wt_scale_win", align_bytes=64)
+        xt_scale_win = keep.tile([P, T], U8, name="xt_scale_win", align_bytes=64)
+        wb_plane = keep.tile([P, N], U8, name="wb_plane", align_bytes=64)
+        nc.vector.memset(wt_scale_win[:].bitcast(I32), 0)
+        nc.vector.memset(xt_scale_win[:].bitcast(I32), 0)
+
+        l2 = load_list(offs2, "l2")
+        wt_word_win = keep.tile([P, F], U16, name="wt_word_win", align_bytes=64)
+        nc.sync.dma_start(out=wt_word_win[:].bitcast(I32), in_=wt_words[0].bitcast(I32))
+        load_scale_rows(nc.scalar, wt_scale_win, wt_scales[0])
+        l1 = load_list(offs, "l1")
+        xt_word_win = keep.tile([P, T], U32, name="xt_word_win", align_bytes=64)
+        nc.sync.dma_start(
+            out=xt_word_win[:].bitcast(I32), in_=xt_words[0].rearrange("p n t -> p (n t)").bitcast(I32)
+        )
+        load_scale_rows(nc.scalar, xt_scale_win, xt_scales[0])
+        l3 = load_list(offs3, "l3")
+        l4 = load_list(offs4, "l4")
+        l5 = load_list(offs5, "l5")
+        l6 = load_list(offs6, "l6")
+        sa_t = keep.tile([P, PACK], F32, name="sa_t")
+        nc.sync.dma_start(out=sa_t[:], in_=sa.rearrange("(p t) o -> p (t o)", t=PACK))
+        sb_t = keep.tile([P, PACK], F32, name="sb_t")
+        nc.sync.dma_start(out=sb_t[:], in_=sb.rearrange("(p t) o -> p (t o)", t=PACK))
+        l7 = load_list(offs7, "l7")
+        wb_w = keep.tile([P, N], U32, name="wb_w", align_bytes=64)
+        nc.sync.dma_start(out=wb_w[:].bitcast(I32), in_=wb_words[0].rearrange("p n t -> p (n t)").bitcast(I32))
+        nc.vector.memset(wb_plane[:].bitcast(I32), 0)
+        load_scale_rows(nc.sync, wb_plane, wb_scales[0])
+
+        pw = [keep.tile([P, C], F32, name="pw0")]
+        pv = [keep.tile([P, C], F32, name="pv0")]
+        nc.vector.memset(pw[0][:], 0.0)
+        nc.vector.memset(pv[0][:], 0.0)
+
+        wt_g = keep.tile([P, R], U16, name="wt_g", align_bytes=64)
+        wt_s = keep.tile([P, R], U8, name="wt_s", align_bytes=64)
+        nc.vector.tensor_copy(out=wt_g[:], in_=wt_word_win[:].indirect(l2[:]))
+        nc.vector.tensor_copy(
+            out=wt_s[:].rearrange("p (t m) -> p m t", t=PACK), in_=wt_scale_win[:].indirect(l2[:])
+        )
+        wt_by_tile = wt_g[:].bitcast(U8).rearrange("p (m t b) -> p t m b", t=PACK, b=2)
+
+        def deal(t):
+            dealt = keep.tile([P, 2 * P], U8, name=f"wt_d{t}", align_bytes=64)
+            nc.vector.tensor_copy(out=dealt[:].rearrange("p (m b) -> p m b", b=2), in_=wt_by_tile[:, t])
+            return dealt
+
+        xt_g = keep.tile([P, J], U32, name="xt_g", align_bytes=64)
+        xt_s = keep.tile([P, J], U8, name="xt_s", align_bytes=64)
+
+        def gather_tokens(lo, hi):
+            nc.vector.tensor_copy(out=xt_g[:, lo:hi], in_=xt_word_win[:].indirect(entries(l1, lo, hi)))
+            nc.vector.tensor_copy(out=xt_s[:, lo:hi], in_=xt_scale_win[:].indirect(entries(l1, lo, hi)))
+
+        def first_product(dealt, t, lo, hi):
+            acc = psum.tile([P, 512], F32, name="acc", tag="acc")
+            nc.tensor.matmul_mx(
+                out=acc[:, : hi - lo],
+                lhsT=dealt[:].bitcast(FP4X4),
+                lhsT_scale=wt_s[:, P * t : P * (t + 1)],
+                rhs=xt_g[:, lo:hi].bitcast(FP8X4),
+                rhs_scale=xt_s[:, lo:hi],
+                start=True,
+                stop=True,
+            )
+            return acc[:, : hi - lo]
+
+        def new_rows(t):
+            a = keep.tile([P, PAD + J], F32, name=f"a{t}", tag=f"slot_w{t}")
+            g = keep.tile([P, J], F32, name=f"g{t}", tag=f"slot_v{t}")
+            nc.gpsimd.memset(a[:, PAD - 1 : PAD], 0.0)
+            return a, g
+
+        def change(a, g, acc, lo, hi):
+            nc.vector.tensor_tensor(out=g[:, lo:hi], in0=acc, in1=a[:, PAD - 1 + lo : PAD - 1 + hi], op=SUB)
+
+        def put(board, lst, src, lo, hi):
+            nc.scalar.activation(out=board[:].indirect(entries(lst, lo, hi)), in_=src, func=COPY)
+
+        def next_board(name, tag):
+            board = keep.tile([P, C], F32, name=name, tag=tag)
+            nc.gpsimd.memset(board[:], 0.0)
+            return board
+
+        hid = [keep.tile([P, HALF, PACK], BF16, name=f"hid{h}", align_bytes=64) for h in range(2)]
+
+        def fetch(t, h):
+            lo, hi = h * HALF, (h + 1) * HALF
+            gw = keep.tile([P, HALF], F32, name="gw", tag="gw", bufs=3)
+            gv = keep.tile([P, HALF], F32, name="gv", tag="gv", bufs=3)
+            nc.scalar.activation(
+                out=gw[:], in_=pw[t][:].indirect(entries(l5, lo, hi)), func=COPY, scale=sa_t[:, t : t + 1]
+            )
+            nc.scalar.activation(
+                out=gv[:], in_=pv[t][:].indirect(entries(l6, lo, hi)), func=COPY, scale=sb_t[:, t : t + 1]
+            )
+            nc.vector.tensor_tensor(out=hid[h][:, :, t], in0=gw[:], in1=gv[:], op=MAX)
+
+        dealt = deal(0)
+        a, g = new_rows(0)
+        gather_tokens(*FIRST_CHUNKS[0])
+        for c, (lo, hi) in enumerate(FIRST_CHUNKS):
+            acc = first_product(dealt, 0, lo, hi)
+            if c == 0:
+                nc.scalar.copy(out=a[:, PAD + lo : PAD + hi], in_=acc)
+            else:
+                nc.vector.tensor_copy(out=a[:, PAD + lo : PAD + hi], in_=acc)
+            if c + 1 < len(FIRST_CHUNKS):
+                gather_tokens(*FIRST_CHUNKS[c + 1])
+            change(a, g, acc, lo, hi)
+            put(pw[0], l3, a[:, PAD + lo : PAD + hi], lo, hi)
+            put(pv[0], l4, g[:, lo:hi], lo, hi)
+
+        for t in range(1, PACK):
+            dealt = deal(t)
+            a, g = new_rows(t)
+            acc = first_product(dealt, t, 0, J)
+            nc.vector.tensor_copy(out=a[:, PAD:], in_=acc)
+            change(a, g, acc, 0, J)
+            fetch(t - 1, 0)
+            pw.append(next_board(f"pw{t}", f"slot_w{t - 1}"))
+            pv.append(next_board(f"pv{t}", f"slot_v{t - 1}"))
+            put(pw[t], l3, a[:, PAD:], 0, J)
+            put(pv[t], l4, g[:], 0, J)
+        fetch(PACK - 1, 0)
+        pages = [next_board("page0", f"slot_w{PACK - 1}"), next_board("page1", f"slot_v{PACK - 1}")]
+
+        def second_product(h):
+            codes = keep.tile([P, HALF], U32, name=f"hid_codes{h}", align_bytes=64)
+            plane = keep.tile([P, HALF], U8, name=f"hid_plane{h}", align_bytes=64)
+            nc.vector.quantize_mx(
+                out=codes[:].bitcast(FP8X4), scales=plane[:], in_=hid[h][:].rearrange("p o t -> p (o t)")
+            )
+            res = []
+            for b in range(N // P):
+                acc = psum.tile([P, 512], F32, name="acc", tag="acc")
+                nc.tensor.matmul_mx(
+                    out=acc[:, :HALF],
+                    lhsT=wb_w[:, P * b : P * (b + 1)].bitcast(FP8X4),
+                    lhsT_scale=wb_plane[:, P * b : P * (b + 1)],
+                    rhs=codes[:].bitcast(FP8X4),
+                    rhs_scale=plane[:],
+                    start=True,
+                    stop=True,
+                )
+                prod = keep.tile([P, HALF], F32, name=f"prod{h}_{b}")
+                nc.vector.tensor_copy(out=prod[:], in_=acc[:, :HALF])
+                res.append(prod)
+            return res
+
+        first = second_product(0)
+        for t in range(PACK):
+            fetch(t, 1)
+        for b in range(N // P):
+            put(pages[b], l7, first[b][:], 0, HALF)
+        second = second_product(1)
+        for b in range(N // P):
+            put(pages[b], l7, second[b][:], HALF, O)
+            page = pages[b]
+            for lo in range(0, U, OUT_CHUNK):
+                hi = lo + OUT_CHUNK
+                step = keep.tile([P, OUT_CHUNK], F32, name=f"step{b}_{lo}")
+                if lo == 0:
+                    nc.vector.tensor_copy(out=step[:, 0:1], in_=page[:, 0:1])
+                    nc.vector.tensor_tensor(out=step[:, 1:], in0=page[:, 1:hi], in1=page[:, 0 : hi - 1], op=SUB)
+                else:
+                    nc.vector.tensor_tensor(out=step[:], in0=page[:, lo:hi], in1=page[:, lo - 1 : hi - 1], op=SUB)
+                nc.sync.dma_start(out=out[P * b : P * (b + 1), lo:hi], in_=step[:])

@@ -21,7 +21,8 @@ P = 128
 PACK = 4
 PAD = 8
 HALF = O // 2
-FIRST_CHUNKS = ((0, 128), (128, 256), (256, 512))
+LEAD = 256
+SLOT_RUNS = ((0, LEAD), (LEAD, J))
 OUT_CHUNK = 256
 
 
@@ -29,9 +30,9 @@ def entries(lst, lo, hi):
     return lst[:, lo // 16 : hi // 16]
 
 
-def load_scale_rows(queue, plane, rows):
+def load_scale_rows(nc, plane, rows):
     for q in range(4):
-        queue.dma_start(out=plane[32 * q : 32 * q + 4, :].bitcast(I32), in_=rows[4 * q : 4 * q + 4, :].bitcast(I32))
+        nc.sync.dma_start(out=plane[32 * q : 32 * q + 4, :].bitcast(I32), in_=rows[4 * q : 4 * q + 4, :].bitcast(I32))
 
 
 def tile_picked_tokens_store_one_changes_one_endsteps_kernel(
@@ -48,35 +49,26 @@ def tile_picked_tokens_store_one_changes_one_endsteps_kernel(
             nc.sync.dma_start(out=tile[:], in_=src)
             return tile
 
-        wt_scale_win = keep.tile([P, F], U8, name="wt_scale_win", align_bytes=64)
-        xt_scale_win = keep.tile([P, T], U8, name="xt_scale_win", align_bytes=64)
-        wb_plane = keep.tile([P, N], U8, name="wb_plane", align_bytes=64)
-        nc.vector.memset(wt_scale_win[:].bitcast(I32), 0)
-        nc.vector.memset(xt_scale_win[:].bitcast(I32), 0)
+        wt_scale_win = keep.tile([P, F], U8, name="wt_scale_win", tag="wt_scale_slot", align_bytes=64)
+        xt_scale_win = keep.tile([P, T], U8, name="xt_scale_win", tag="xt_scale_slot", align_bytes=64)
+        nc.gpsimd.memset(wt_scale_win[:].bitcast(I32), 0)
+        nc.gpsimd.memset(xt_scale_win[:].bitcast(I32), 0)
 
-        l2 = load_list(offs2, "l2")
-        wt_word_win = keep.tile([P, F], U16, name="wt_word_win", align_bytes=64)
+        wt_word_win = keep.tile([P, F], U16, name="wt_word_win", tag="wt_word_slot", align_bytes=64)
         nc.sync.dma_start(out=wt_word_win[:].bitcast(I32), in_=wt_words[0].bitcast(I32))
-        load_scale_rows(nc.scalar, wt_scale_win, wt_scales[0])
-        l1 = load_list(offs, "l1")
-        xt_word_win = keep.tile([P, T], U32, name="xt_word_win", align_bytes=64)
+        l2 = load_list(offs2, "l2")
+        xt_word_win = keep.tile([P, T], U32, name="xt_word_win", tag="xt_word_slot", align_bytes=64)
         nc.sync.dma_start(
             out=xt_word_win[:].bitcast(I32), in_=xt_words[0].rearrange("p n t -> p (n t)").bitcast(I32)
         )
-        load_scale_rows(nc.scalar, xt_scale_win, xt_scales[0])
+        l1 = load_list(offs, "l1")
+        load_scale_rows(nc, wt_scale_win, wt_scales[0])
+        load_scale_rows(nc, xt_scale_win, xt_scales[0])
         l3 = load_list(offs3, "l3")
         l4 = load_list(offs4, "l4")
         l5 = load_list(offs5, "l5")
         l6 = load_list(offs6, "l6")
-        sa_t = keep.tile([P, PACK], F32, name="sa_t")
-        nc.sync.dma_start(out=sa_t[:], in_=sa.rearrange("(p t) o -> p (t o)", t=PACK))
-        sb_t = keep.tile([P, PACK], F32, name="sb_t")
-        nc.sync.dma_start(out=sb_t[:], in_=sb.rearrange("(p t) o -> p (t o)", t=PACK))
         l7 = load_list(offs7, "l7")
-        wb_w = keep.tile([P, N], U32, name="wb_w", align_bytes=64)
-        nc.sync.dma_start(out=wb_w[:].bitcast(I32), in_=wb_words[0].rearrange("p n t -> p (n t)").bitcast(I32))
-        nc.vector.memset(wb_plane[:].bitcast(I32), 0)
-        load_scale_rows(nc.sync, wb_plane, wb_scales[0])
 
         pw = [keep.tile([P, C], F32, name="pw0")]
         pv = [keep.tile([P, C], F32, name="pv0")]
@@ -86,107 +78,126 @@ def tile_picked_tokens_store_one_changes_one_endsteps_kernel(
         wt_g = keep.tile([P, R], U16, name="wt_g", align_bytes=64)
         wt_s = keep.tile([P, R], U8, name="wt_s", align_bytes=64)
         nc.vector.tensor_copy(out=wt_g[:], in_=wt_word_win[:].indirect(l2[:]))
+        wt_by_tile = wt_g[:].bitcast(U8).rearrange("p (m t b) -> p t m b", t=PACK, b=2)
+        dealt_first = keep.tile([P, 2 * P], U8, name="dealt_first", align_bytes=64)
+        nc.vector.tensor_copy(out=dealt_first[:].rearrange("p (m b) -> p m b", b=2), in_=wt_by_tile[:, 0])
         nc.vector.tensor_copy(
             out=wt_s[:].rearrange("p (t m) -> p m t", t=PACK), in_=wt_scale_win[:].indirect(l2[:])
         )
-        wt_by_tile = wt_g[:].bitcast(U8).rearrange("p (m t b) -> p t m b", t=PACK, b=2)
 
-        def deal(t):
-            dealt = keep.tile([P, 2 * P], U8, name=f"wt_d{t}", align_bytes=64)
-            nc.vector.tensor_copy(out=dealt[:].rearrange("p (m b) -> p m b", b=2), in_=wt_by_tile[:, t])
-            return dealt
+        lead_words = keep.tile([P, LEAD], U32, name="lead_words", align_bytes=64)
+        lead_scales = keep.tile([P, LEAD], U8, name="lead_scales", align_bytes=64)
+        nc.vector.tensor_copy(out=lead_words[:], in_=xt_word_win[:].indirect(entries(l1, 0, LEAD)))
+        nc.vector.tensor_copy(out=lead_scales[:], in_=xt_scale_win[:].indirect(entries(l1, 0, LEAD)))
+        rest_scales = keep.tile([P, J - LEAD], U8, name="rest_scales", align_bytes=64)
+        nc.vector.tensor_copy(out=rest_scales[:], in_=xt_scale_win[:].indirect(entries(l1, LEAD, J)))
+        rest_words = keep.tile([P, J - LEAD], U32, name="rest_words", tag="xt_scale_slot", align_bytes=64)
+        nc.vector.tensor_copy(out=rest_words[:], in_=xt_word_win[:].indirect(entries(l1, LEAD, J)))
 
-        xt_g = keep.tile([P, J], U32, name="xt_g", align_bytes=64)
-        xt_s = keep.tile([P, J], U8, name="xt_s", align_bytes=64)
-
-        def gather_tokens(lo, hi):
-            nc.vector.tensor_copy(out=xt_g[:, lo:hi], in_=xt_word_win[:].indirect(entries(l1, lo, hi)))
-            nc.vector.tensor_copy(out=xt_s[:, lo:hi], in_=xt_scale_win[:].indirect(entries(l1, lo, hi)))
-
-        def first_product(dealt, t, lo, hi):
-            acc = psum.tile([P, 512], F32, name="acc", tag="acc")
+        def first_product(acc, dealt, t, lo, hi):
+            if lo < LEAD:
+                words, scales = lead_words[:], lead_scales[:]
+            else:
+                words, scales = rest_words[:, lo - LEAD : hi - LEAD], rest_scales[:, lo - LEAD : hi - LEAD]
             nc.tensor.matmul_mx(
-                out=acc[:, : hi - lo],
-                lhsT=dealt[:].bitcast(FP4X4),
+                out=acc,
+                lhsT=dealt.bitcast(FP4X4),
                 lhsT_scale=wt_s[:, P * t : P * (t + 1)],
-                rhs=xt_g[:, lo:hi].bitcast(FP8X4),
-                rhs_scale=xt_s[:, lo:hi],
+                rhs=words.bitcast(FP8X4),
+                rhs_scale=scales,
                 start=True,
                 stop=True,
             )
-            return acc[:, : hi - lo]
 
-        def new_rows(t):
-            a = keep.tile([P, PAD + J], F32, name=f"a{t}", tag=f"slot_w{t}")
-            g = keep.tile([P, J], F32, name=f"g{t}", tag=f"slot_v{t}")
+        def new_values(t):
+            a = keep.tile([P, PAD + J], F32, name=f"a{t}", tag=f"slot_w{t}", align_bytes=64)
             nc.gpsimd.memset(a[:, PAD - 1 : PAD], 0.0)
-            return a, g
-
-        def change(a, g, acc, lo, hi):
-            nc.vector.tensor_tensor(out=g[:, lo:hi], in0=acc, in1=a[:, PAD - 1 + lo : PAD - 1 + hi], op=SUB)
+            return a
 
         def put(board, lst, src, lo, hi):
             nc.scalar.activation(out=board[:].indirect(entries(lst, lo, hi)), in_=src, func=COPY)
 
         def next_board(name, tag):
-            board = keep.tile([P, C], F32, name=name, tag=tag)
+            board = keep.tile([P, C], F32, name=name, tag=tag, align_bytes=64)
             nc.gpsimd.memset(board[:], 0.0)
             return board
 
+        a = new_values(0)
+        lead_bank = psum.tile([P, 512], F32, name="bank", tag="bank")
+        first_product(lead_bank[:, :LEAD], dealt_first[:], 0, 0, LEAD)
+        lead_g = keep.tile([P, LEAD], F32, name="lead_g")
+        nc.scalar.copy(out=a[:, PAD : PAD + LEAD], in_=lead_bank[:, :LEAD])
+        nc.vector.tensor_tensor(
+            out=lead_g[:], in0=lead_bank[:, :LEAD], in1=a[:, PAD - 1 : PAD - 1 + LEAD], op=SUB
+        )
+        put(pw[0], l3, a[:, PAD : PAD + LEAD], 0, LEAD)
+        put(pv[0], l4, lead_g[:], 0, LEAD)
+        rest_bank = psum.tile([P, 512], F32, name="bank", tag="bank")
+        for lo, hi in SLOT_RUNS[1:]:
+            first_product(rest_bank[:, lo:hi], dealt_first[:], 0, lo, hi)
+        rest_g = keep.tile([P, J - LEAD], F32, name="rest_g", tag="slot_v0", align_bytes=64)
+        nc.vector.tensor_copy(out=a[:, PAD + LEAD :], in_=rest_bank[:, LEAD:])
+        nc.vector.tensor_tensor(
+            out=rest_g[:], in0=rest_bank[:, LEAD:], in1=a[:, PAD - 1 + LEAD : PAD - 1 + J], op=SUB
+        )
+        put(pw[0], l3, a[:, PAD + LEAD :], LEAD, J)
+        put(pv[0], l4, rest_g[:], LEAD, J)
+
+        weights = keep.tile([P, 16], F32, name="weights", tag="wt_scale_slot", align_bytes=64)
+        nc.sync.dma_start(out=weights[:, 0:PACK], in_=sa.rearrange("(p t) o -> p (t o)", t=PACK))
+        nc.sync.dma_start(out=weights[:, 8 : 8 + PACK], in_=sb.rearrange("(p t) o -> p (t o)", t=PACK))
+        dealt_rest = keep.tile([P, PACK - 1, 2 * P], U8, name="dealt_rest", tag="xt_word_slot", align_bytes=64)
+        nc.vector.tensor_copy(out=dealt_rest[:].rearrange("p t (m b) -> p t m b", b=2), in_=wt_by_tile[:, 1:])
+
         hid = [keep.tile([P, HALF, PACK], BF16, name=f"hid{h}", align_bytes=64) for h in range(2)]
 
-        def fetch(t, h):
-            lo, hi = h * HALF, (h + 1) * HALF
-            gw = keep.tile([P, HALF], F32, name="gw", tag="gw", bufs=3)
-            gv = keep.tile([P, HALF], F32, name="gv", tag="gv", bufs=3)
+        def fetch(t, lo, hi, tag_w, tag_v, targets):
+            gw = keep.tile([P, hi - lo], F32, name=f"gw{t}_{lo}", tag=tag_w, align_bytes=64)
+            gv = keep.tile([P, hi - lo], F32, name=f"gv{t}_{lo}", tag=tag_v, align_bytes=64)
             nc.scalar.activation(
-                out=gw[:], in_=pw[t][:].indirect(entries(l5, lo, hi)), func=COPY, scale=sa_t[:, t : t + 1]
+                out=gw[:], in_=pw[t][:].indirect(entries(l5, lo, hi)), func=COPY, scale=weights[:, t : t + 1]
             )
             nc.scalar.activation(
-                out=gv[:], in_=pv[t][:].indirect(entries(l6, lo, hi)), func=COPY, scale=sb_t[:, t : t + 1]
+                out=gv[:], in_=pv[t][:].indirect(entries(l6, lo, hi)), func=COPY, scale=weights[:, 8 + t : 9 + t]
             )
-            nc.vector.tensor_tensor(out=hid[h][:, :, t], in0=gw[:], in1=gv[:], op=MAX)
+            for i, target in enumerate(targets):
+                cols = slice(i * HALF, (i + 1) * HALF)
+                nc.vector.tensor_tensor(out=target, in0=gw[:, cols], in1=gv[:, cols], op=MAX)
 
-        dealt = deal(0)
-        a, g = new_rows(0)
-        gather_tokens(*FIRST_CHUNKS[0])
-        for c, (lo, hi) in enumerate(FIRST_CHUNKS):
-            acc = first_product(dealt, 0, lo, hi)
-            if c == 0:
-                nc.scalar.copy(out=a[:, PAD + lo : PAD + hi], in_=acc)
-            else:
-                nc.vector.tensor_copy(out=a[:, PAD + lo : PAD + hi], in_=acc)
-            if c + 1 < len(FIRST_CHUNKS):
-                gather_tokens(*FIRST_CHUNKS[c + 1])
-            change(a, g, acc, lo, hi)
-            put(pw[0], l3, a[:, PAD + lo : PAD + hi], lo, hi)
-            put(pv[0], l4, g[:, lo:hi], lo, hi)
-
+        last = PACK - 1
         for t in range(1, PACK):
-            dealt = deal(t)
-            a, g = new_rows(t)
-            acc = first_product(dealt, t, 0, J)
-            nc.vector.tensor_copy(out=a[:, PAD:], in_=acc)
-            change(a, g, acc, 0, J)
-            fetch(t - 1, 0)
-            pw.append(next_board(f"pw{t}", f"slot_w{t - 1}"))
-            pv.append(next_board(f"pv{t}", f"slot_v{t - 1}"))
+            a = new_values(t)
+            g = keep.tile([P, J], F32, name=f"g{t}", tag=f"slot_v{t}", align_bytes=64)
+            bank = psum.tile([P, 512], F32, name="bank", tag="bank")
+            for lo, hi in SLOT_RUNS:
+                first_product(bank[:, lo:hi], dealt_rest[:, t - 1, :], t, lo, hi)
+            nc.vector.tensor_copy(out=a[:, PAD:], in_=bank[:])
+            nc.vector.tensor_tensor(out=g[:], in0=bank[:], in1=a[:, PAD - 1 : PAD - 1 + J], op=SUB)
+            halves = hid[:1] if t == last else hid
+            fetch(t - 1, 0, HALF * len(halves), f"slot_gw{t - 1}", f"slot_gv{t - 1}", [x[:, :, t - 1] for x in halves])
+            pw.append(next_board("pw_last", "slot_w0") if t == last else pw[0])
+            pv.append(next_board("pv_last", "slot_v0") if t == last else pv[0])
             put(pw[t], l3, a[:, PAD:], 0, J)
             put(pv[t], l4, g[:], 0, J)
-        fetch(PACK - 1, 0)
-        pages = [next_board("page0", f"slot_w{PACK - 1}"), next_board("page1", f"slot_v{PACK - 1}")]
+        fetch(last, 0, HALF, "slot_gw3", "slot_gv3", [hid[0][:, :, last]])
+        pages = [next_board("page0", "slot_w1"), next_board("page1", "slot_v1")]
+        wb_w = keep.tile([P, N], U32, name="wb_w", tag="wt_word_slot", align_bytes=64)
+        nc.sync.dma_start(out=wb_w[:].bitcast(I32), in_=wb_words[0].rearrange("p n t -> p (n t)").bitcast(I32))
+        wb_plane = keep.tile([P, N], U8, name="wb_plane", tag="xt_scale_slot", align_bytes=64)
+        nc.gpsimd.memset(wb_plane[:].bitcast(I32), 0)
+        load_scale_rows(nc, wb_plane, wb_scales[0])
 
         def second_product(h):
-            codes = keep.tile([P, HALF], U32, name=f"hid_codes{h}", align_bytes=64)
+            codes = keep.tile([P, HALF], U32, name=f"hid_codes{h}", tag=f"slot_codes{h}", align_bytes=64)
             plane = keep.tile([P, HALF], U8, name=f"hid_plane{h}", align_bytes=64)
             nc.vector.quantize_mx(
                 out=codes[:].bitcast(FP8X4), scales=plane[:], in_=hid[h][:].rearrange("p o t -> p (o t)")
             )
             res = []
             for b in range(N // P):
-                acc = psum.tile([P, 512], F32, name="acc", tag="acc")
+                bank = psum.tile([P, 512], F32, name="bank", tag="bank")
                 nc.tensor.matmul_mx(
-                    out=acc[:, :HALF],
+                    out=bank[:, :HALF],
                     lhsT=wb_w[:, P * b : P * (b + 1)].bitcast(FP8X4),
                     lhsT_scale=wb_plane[:, P * b : P * (b + 1)],
                     rhs=codes[:].bitcast(FP8X4),
@@ -195,13 +206,15 @@ def tile_picked_tokens_store_one_changes_one_endsteps_kernel(
                     stop=True,
                 )
                 prod = keep.tile([P, HALF], F32, name=f"prod{h}_{b}")
-                nc.vector.tensor_copy(out=prod[:], in_=acc[:, :HALF])
+                nc.vector.tensor_copy(out=prod[:], in_=bank[:, :HALF])
                 res.append(prod)
             return res
 
         first = second_product(0)
-        for t in range(PACK):
-            fetch(t, 1)
+        late = keep.tile([P, HALF, 2], BF16, name="late", tag="slot_codes0", align_bytes=64)
+        fetch(last - 1, HALF, O, f"slot_w{last}", f"slot_v{last}", [late[:, :, 0]])
+        fetch(last, HALF, O, "slot_gw3_late", "slot_gv3_late", [late[:, :, 1]])
+        nc.vector.tensor_copy(out=hid[1][:].bitcast(F32)[:, :, 1:2], in_=late[:].bitcast(F32))
         for b in range(N // P):
             put(pages[b], l7, first[b][:], 0, HALF)
         second = second_product(1)

from contextlib import ExitStack

import concourse.mybir as mybir

K, J, R, T, F, C, O, N, U = 512, 512, 512, 1024, 1024, 1024, 512, 256, 1024
FLOPS = 2 * K * R * J + 2 * R * N * O

F32 = mybir.dt.float32
BF16 = mybir.dt.bfloat16
I32 = mybir.dt.int32
U32 = mybir.dt.uint32
U16 = mybir.dt.uint16
U8 = mybir.dt.uint8
FP8X4 = mybir.dt.float8_e4m3fn_x4
FP4X4 = mybir.dt.float4_e2m1fn_x4
COPY = mybir.ActivationFunctionType.Copy
SUB = mybir.AluOpType.subtract
MAX = mybir.AluOpType.max

P = 128
PACK = 4
PAD = 8
HALF = O // 2
LEAD = 256
SLOT_RUNS = ((0, LEAD), (LEAD, J))
OUT_CHUNK = 256


def entries(lst, lo, hi):
    return lst[:, lo // 16 : hi // 16]


def load_scale_rows(nc, plane, rows):
    for q in range(4):
        nc.sync.dma_start(out=plane[32 * q : 32 * q + 4, :].bitcast(I32), in_=rows[4 * q : 4 * q + 4, :].bitcast(I32))


def tile_picked_tokens_store_one_changes_one_endsteps_kernel(
    tc, xt_words, xt_scales, wt_words, wt_scales, sa, sb, wb_words, wb_scales,
    offs, offs2, offs3, offs4, offs5, offs6, offs7, out,
):
    nc = tc.nc
    with ExitStack() as ctx:
        keep = ctx.enter_context(tc.tile_pool(name="keep", bufs=1))
        psum = ctx.enter_context(tc.psum_pool(name="psum", bufs=8))

        def load_list(src, name):
            tile = keep.tile([P, 32], U16, name=name)
            nc.sync.dma_start(out=tile[:], in_=src)
            return tile

        wt_scale_win = keep.tile([P, F], U8, name="wt_scale_win", tag="wt_scale_slot", align_bytes=64)
        xt_scale_win = keep.tile([P, T], U8, name="xt_scale_win", tag="xt_scale_slot", align_bytes=64)
        nc.gpsimd.memset(wt_scale_win[:].bitcast(I32), 0)
        nc.gpsimd.memset(xt_scale_win[:].bitcast(I32), 0)

        wt_word_win = keep.tile([P, F], U16, name="wt_word_win", tag="wt_word_slot", align_bytes=64)
        nc.sync.dma_start(out=wt_word_win[:].bitcast(I32), in_=wt_words[0].bitcast(I32))
        l2 = load_list(offs2, "l2")
        xt_word_win = keep.tile([P, T], U32, name="xt_word_win", tag="xt_word_slot", align_bytes=64)
        nc.sync.dma_start(
            out=xt_word_win[:].bitcast(I32), in_=xt_words[0].rearrange("p n t -> p (n t)").bitcast(I32)
        )
        l1 = load_list(offs, "l1")
        load_scale_rows(nc, wt_scale_win, wt_scales[0])
        load_scale_rows(nc, xt_scale_win, xt_scales[0])
        l3 = load_list(offs3, "l3")
        l4 = load_list(offs4, "l4")
        l5 = load_list(offs5, "l5")
        l6 = load_list(offs6, "l6")
        l7 = load_list(offs7, "l7")

        pw = [keep.tile([P, C], F32, name="pw0")]
        pv = [keep.tile([P, C], F32, name="pv0")]
        nc.vector.memset(pw[0][:], 0.0)
        nc.vector.memset(pv[0][:], 0.0)

        wt_g = keep.tile([P, R], U16, name="wt_g", align_bytes=64)
        wt_s = keep.tile([P, R], U8, name="wt_s", align_bytes=64)
        nc.vector.tensor_copy(out=wt_g[:], in_=wt_word_win[:].indirect(l2[:]))
        wt_by_tile = wt_g[:].bitcast(U8).rearrange("p (m t b) -> p t m b", t=PACK, b=2)
        dealt_first = keep.tile([P, 2 * P], U8, name="dealt_first", align_bytes=64)
        nc.vector.tensor_copy(out=dealt_first[:].rearrange("p (m b) -> p m b", b=2), in_=wt_by_tile[:, 0])
        nc.vector.tensor_copy(
            out=wt_s[:].rearrange("p (t m) -> p m t", t=PACK), in_=wt_scale_win[:].indirect(l2[:])
        )

        lead_words = keep.tile([P, LEAD], U32, name="lead_words", align_bytes=64)
        lead_scales = keep.tile([P, LEAD], U8, name="lead_scales", align_bytes=64)
        nc.vector.tensor_copy(out=lead_words[:], in_=xt_word_win[:].indirect(entries(l1, 0, LEAD)))
        nc.vector.tensor_copy(out=lead_scales[:], in_=xt_scale_win[:].indirect(entries(l1, 0, LEAD)))
        rest_scales = keep.tile([P, J - LEAD], U8, name="rest_scales", align_bytes=64)
        nc.vector.tensor_copy(out=rest_scales[:], in_=xt_scale_win[:].indirect(entries(l1, LEAD, J)))
        rest_words = keep.tile([P, J - LEAD], U32, name="rest_words", tag="xt_scale_slot", align_bytes=64)
        nc.vector.tensor_copy(out=rest_words[:], in_=xt_word_win[:].indirect(entries(l1, LEAD, J)))

        def first_product(acc, dealt, t, lo, hi):
            if lo < LEAD:
                words, scales = lead_words[:], lead_scales[:]
            else:
                words, scales = rest_words[:, lo - LEAD : hi - LEAD], rest_scales[:, lo - LEAD : hi - LEAD]
            nc.tensor.matmul_mx(
                out=acc,
                lhsT=dealt.bitcast(FP4X4),
                lhsT_scale=wt_s[:, P * t : P * (t + 1)],
                rhs=words.bitcast(FP8X4),
                rhs_scale=scales,
                start=True,
                stop=True,
            )

        def new_values(t):
            a = keep.tile([P, PAD + J], F32, name=f"a{t}", tag=f"slot_w{t}", align_bytes=64)
            nc.gpsimd.memset(a[:, PAD - 1 : PAD], 0.0)
            return a

        def put(board, lst, src, lo, hi):
            nc.scalar.activation(out=board[:].indirect(entries(lst, lo, hi)), in_=src, func=COPY)

        def next_board(name, tag):
            board = keep.tile([P, C], F32, name=name, tag=tag, align_bytes=64)
            nc.gpsimd.memset(board[:], 0.0)
            return board

        a = new_values(0)
        lead_bank = psum.tile([P, 512], F32, name="bank", tag="bank")
        first_product(lead_bank[:, :LEAD], dealt_first[:], 0, 0, LEAD)
        lead_g = keep.tile([P, LEAD], F32, name="lead_g")
        nc.scalar.copy(out=a[:, PAD : PAD + LEAD], in_=lead_bank[:, :LEAD])
        nc.vector.tensor_tensor(
            out=lead_g[:], in0=lead_bank[:, :LEAD], in1=a[:, PAD - 1 : PAD - 1 + LEAD], op=SUB
        )
        put(pw[0], l3, a[:, PAD : PAD + LEAD], 0, LEAD)
        put(pv[0], l4, lead_g[:], 0, LEAD)
        rest_bank = psum.tile([P, 512], F32, name="bank", tag="bank")
        for lo, hi in SLOT_RUNS[1:]:
            first_product(rest_bank[:, lo:hi], dealt_first[:], 0, lo, hi)
        rest_g = keep.tile([P, J - LEAD], F32, name="rest_g", tag="slot_v0", align_bytes=64)
        nc.vector.tensor_copy(out=a[:, PAD + LEAD :], in_=rest_bank[:, LEAD:])
        nc.vector.tensor_tensor(
            out=rest_g[:], in0=rest_bank[:, LEAD:], in1=a[:, PAD - 1 + LEAD : PAD - 1 + J], op=SUB
        )
        put(pw[0], l3, a[:, PAD + LEAD :], LEAD, J)
        put(pv[0], l4, rest_g[:], LEAD, J)

        weights = keep.tile([P, 16], F32, name="weights", tag="wt_scale_slot", align_bytes=64)
        nc.sync.dma_start(out=weights[:, 0:PACK], in_=sa.rearrange("(p t) o -> p (t o)", t=PACK))
        nc.sync.dma_start(out=weights[:, 8 : 8 + PACK], in_=sb.rearrange("(p t) o -> p (t o)", t=PACK))
        dealt_rest = keep.tile([P, PACK - 1, 2 * P], U8, name="dealt_rest", tag="xt_word_slot", align_bytes=64)
        nc.vector.tensor_copy(out=dealt_rest[:].rearrange("p t (m b) -> p t m b", b=2), in_=wt_by_tile[:, 1:])

        hid = [keep.tile([P, HALF, PACK], BF16, name=f"hid{h}", align_bytes=64) for h in range(2)]

        def fetch(t, lo, hi, tag_w, tag_v, targets):
            gw = keep.tile([P, hi - lo], F32, name=f"gw{t}_{lo}", tag=tag_w, align_bytes=64)
            gv = keep.tile([P, hi - lo], F32, name=f"gv{t}_{lo}", tag=tag_v, align_bytes=64)
            nc.scalar.activation(
                out=gw[:], in_=pw[t][:].indirect(entries(l5, lo, hi)), func=COPY, scale=weights[:, t : t + 1]
            )
            nc.scalar.activation(
                out=gv[:], in_=pv[t][:].indirect(entries(l6, lo, hi)), func=COPY, scale=weights[:, 8 + t : 9 + t]
            )
            for i, target in enumerate(targets):
                cols = slice(i * HALF, (i + 1) * HALF)
                nc.vector.tensor_tensor(out=target, in0=gw[:, cols], in1=gv[:, cols], op=MAX)

        last = PACK - 1
        for t in range(1, PACK):
            a = new_values(t)
            g = keep.tile([P, J], F32, name=f"g{t}", tag=f"slot_v{t}", align_bytes=64)
            bank = psum.tile([P, 512], F32, name="bank", tag="bank")
            for lo, hi in SLOT_RUNS:
                first_product(bank[:, lo:hi], dealt_rest[:, t - 1, :], t, lo, hi)
            nc.vector.tensor_copy(out=a[:, PAD:], in_=bank[:])
            nc.vector.tensor_tensor(out=g[:], in0=bank[:], in1=a[:, PAD - 1 : PAD - 1 + J], op=SUB)
            halves = hid[:1] if t == last else hid
            fetch(t - 1, 0, HALF * len(halves), f"slot_gw{t - 1}", f"slot_gv{t - 1}", [x[:, :, t - 1] for x in halves])
            pw.append(next_board("pw_last", "slot_w0") if t == last else pw[0])
            pv.append(next_board("pv_last", "slot_v0") if t == last else pv[0])
            put(pw[t], l3, a[:, PAD:], 0, J)
            put(pv[t], l4, g[:], 0, J)
        fetch(last, 0, HALF, "slot_gw3", "slot_gv3", [hid[0][:, :, last]])
        pages = [next_board("page0", "slot_w1"), next_board("page1", "slot_v1")]
        wb_w = keep.tile([P, N], U32, name="wb_w", tag="wt_word_slot", align_bytes=64)
        nc.sync.dma_start(out=wb_w[:].bitcast(I32), in_=wb_words[0].rearrange("p n t -> p (n t)").bitcast(I32))
        wb_plane = keep.tile([P, N], U8, name="wb_plane", tag="xt_scale_slot", align_bytes=64)
        nc.gpsimd.memset(wb_plane[:].bitcast(I32), 0)
        load_scale_rows(nc, wb_plane, wb_scales[0])

        def second_product(h):
            codes = keep.tile([P, HALF], U32, name=f"hid_codes{h}", tag=f"slot_codes{h}", align_bytes=64)
            plane = keep.tile([P, HALF], U8, name=f"hid_plane{h}", align_bytes=64)
            nc.vector.quantize_mx(
                out=codes[:].bitcast(FP8X4), scales=plane[:], in_=hid[h][:].rearrange("p o t -> p (o t)")
            )
            res = []
            for b in range(N // P):
                bank = psum.tile([P, 512], F32, name="bank", tag="bank")
                nc.tensor.matmul_mx(
                    out=bank[:, :HALF],
                    lhsT=wb_w[:, P * b : P * (b + 1)].bitcast(FP8X4),
                    lhsT_scale=wb_plane[:, P * b : P * (b + 1)],
                    rhs=codes[:].bitcast(FP8X4),
                    rhs_scale=plane[:],
                    start=True,
                    stop=True,
                )
                prod = keep.tile([P, HALF], F32, name=f"prod{h}_{b}")
                nc.vector.tensor_copy(out=prod[:], in_=bank[:, :HALF])
                res.append(prod)
            return res

        first = second_product(0)
        late = keep.tile([P, HALF, 2], BF16, name="late", tag="slot_codes0", align_bytes=64)
        fetch(last - 1, HALF, O, f"slot_w{last}", f"slot_v{last}", [late[:, :, 0]])
        fetch(last, HALF, O, "slot_gw3_late", "slot_gv3_late", [late[:, :, 1]])
        nc.vector.tensor_copy(out=hid[1][:].bitcast(F32)[:, :, 1:2], in_=late[:].bitcast(F32))
        for b in range(N // P):
            put(pages[b], l7, first[b][:], 0, HALF)
        second = second_product(1)
        for b in range(N // P):
            put(pages[b], l7, second[b][:], HALF, O)
            page = pages[b]
            for lo in range(0, U, OUT_CHUNK):
                hi = lo + OUT_CHUNK
                step = keep.tile([P, OUT_CHUNK], F32, name=f"step{b}_{lo}")
                if lo == 0:
                    nc.vector.tensor_copy(out=step[:, 0:1], in_=page[:, 0:1])
                    nc.vector.tensor_tensor(out=step[:, 1:], in0=page[:, 1:hi], in1=page[:, 0 : hi - 1], op=SUB)
                else:
                    nc.vector.tensor_tensor(out=step[:], in0=page[:, lo:hi], in1=page[:, lo - 1 : hi - 1], op=SUB)
                nc.sync.dma_start(out=out[P * b : P * (b + 1), lo:hi], in_=step[:])
